import numpy as np
import ml_dtypes


def mxq(x, axis, fmt="e4m3"):
    dtype, down = {"e4m3": (ml_dtypes.float8_e4m3fn, 7), "e5m2": (ml_dtypes.float8_e5m2, 14)}[fmt]
    v = np.moveaxis(np.asarray(x, np.float32).astype(ml_dtypes.bfloat16).astype(np.float64), axis, -1)
    blocks = v.reshape(v.shape[:-1] + (-1, 32))
    amax = np.abs(blocks).max(-1, keepdims=True)
    byte = np.maximum(np.where(amax > 0, np.frexp(amax)[1] - 1 + 127, 0) - down, 1)
    scale = np.exp2(byte - 127.0)
    codes = (blocks / scale).astype(np.float32).astype(dtype).astype(np.float64)
    return np.moveaxis((codes * scale).reshape(v.shape), -1, axis)


WIDE = False


def mx_kscale(k):
    if not WIDE:
        return np.ones(k)
    levels = np.array([10, -10, 5, -5, 0])
    if k % 512:
        return np.exp2(np.random.permutation(np.resize(levels, k // 32))).repeat(32)
    a = np.empty((k // 512, 16))
    for p in range(k // 512):
        a[p, :8] = np.random.permutation(np.resize(levels, 8))
        for g in range(8):
            far = levels[np.abs(levels - a[p, g]) >= 10]
            a[p, g + 8] = far[np.random.randint(len(far))]
    return np.exp2(a.ravel()).repeat(32)


def f64(x):
    return np.asarray(x).astype(np.float64)


def striped(idx):
    return np.tile(idx.reshape(-1, 16).T, (8, 1)).astype(np.uint16)


def unstriped(offs):
    return offs[:16].T.reshape(-1).astype(np.int64)


E2M1 = np.array([0.0, 0.5, 1.0, 1.5, 2.0, 3.0, 4.0, 6.0, -0.0, -0.5, -1.0, -1.5, -2.0, -3.0, -4.0, -6.0])


def pack_weight(w, fmt):
    k, n = w.shape
    w = f64(np.asarray(w, np.float32).astype(ml_dtypes.bfloat16)).reshape(k // 32, 32, n)
    amax = np.abs(w).max(1)
    if fmt == "e4m3":
        byte = np.frexp(amax)[1] - 1 + 127 - 7
    else:
        mant, ex = np.frexp(amax / 6.0)
        byte = np.where(mant > 0.5, ex, ex - 1) + 127
    byte = np.clip(np.where(amax > 0, byte, 1), 1, 254)
    scaled = (w * np.exp2(127.0 - byte)[:, None, :]).reshape(k, n).astype(np.float32)
    by_word = np.ascontiguousarray(scaled.reshape(k // 512, 128, 4, n).transpose(0, 1, 3, 2))
    if fmt == "e4m3":
        words = by_word.astype(ml_dtypes.float8_e4m3fn).view(np.uint8)
    else:
        c = by_word.astype(ml_dtypes.float4_e2m1fn).view(np.uint8) & 0xF
        words = (c[..., 0::2] | (c[..., 1::2] << 4)).reshape(k // 512, 128, 2 * n)
    return np.ascontiguousarray(words), np.ascontiguousarray(byte.astype(np.uint8).reshape(k // 512, 16, n))


def unpack_weight(words, scales, fmt):
    g, _, n = scales.shape
    words = np.ascontiguousarray(words).reshape(g, 128, n, -1)
    if fmt == "e4m3":
        vals = words.view(ml_dtypes.float8_e4m3fn).astype(np.float64)
    else:
        nib = np.empty((g, 128, n, 4), np.uint8)
        nib[..., 0::2] = words & 0xF
        nib[..., 1::2] = words >> 4
        vals = E2M1[nib]
    vals = vals * np.repeat(np.exp2(scales.astype(np.float64) - 127.0), 8, axis=1)[..., None]
    return vals.transpose(0, 1, 3, 2).reshape(g * 512, n)


def gelu(v):
    return 0.5 * v * (1.0 + np.tanh(np.sqrt(2.0 / np.pi) * (v + 0.044715 * v**3)))


K, T, S, S2 = 1024, 2048, 1024, 512

def setup_inputs():
    n = np.random.standard_normal
    s = mx_kscale(K)[:, None]
    d = {}
    d["tab_words"], d["tab_scales"] = pack_weight(n((K, T)) * s, "e4m3")
    d["offs"] = striped(np.random.permutation(T)[:S])
    d["offs2"] = striped(np.random.permutation(T)[:S2])
    d["w1"] = (2.5 * n((K, K)) / K ** 0.5 / s).astype(np.float32)
    d["w4_words"], d["w4_scales"] = pack_weight(1.3 * n((K, K)) / K ** 0.5 / s, "e2m1")
    d["ref"] = (0.8 * n(K)).astype(np.float32)
    d["gain"] = (1.2 * n(K) / K ** 0.5 / s[:, 0]).astype(np.float32)
    d["house"] = np.exp(0.4 * n(S2)).astype(np.float32)
    d["visit"] = (0.6 * n((S2, S))).astype(np.float32)
    return d

def reference(tab_words, tab_scales, offs, offs2, w1, w4_words, w4_scales, ref, gain, house, visit):
    TW = unpack_weight(tab_words, tab_scales, "e4m3")
    v = TW[:, unstriped(offs)]
    v2 = TW[:, unstriped(offs2)]
    w4 = unpack_weight(w4_words, w4_scales, "e2m1")
    arg = mxq(f64(w1), 0, "e4m3").T @ v
    gate = 1.0 / (1.0 + np.exp(-arg))
    trait = w4.T @ v
    dev = np.abs(trait - f64(ref)[:, None])
    h = f64(gain)[:, None] * (gate * dev)
    e = v2.T @ mxq(h, 0, "e4m3")
    return f64(house)[:, None] * e + f64(visit)

@@ -1,0 +1,282 @@
+from contextlib import ExitStack
+
+import concourse.mybir as mybir
+
+K, T, S, S2 = 1024, 2048, 1024, 512
+FLOPS = 2 * K * K * S * 2 + 2 * K * S2 * S
+
+F32 = mybir.dt.float32
+BF16 = mybir.dt.bfloat16
+I32 = mybir.dt.int32
+U32 = mybir.dt.uint32
+U16 = mybir.dt.uint16
+U8 = mybir.dt.uint8
+FP8X4 = mybir.dt.float8_e4m3fn_x4
+FP4X4 = mybir.dt.float4_e2m1fn_x4
+ACT = mybir.ActivationFunctionType
+ALU = mybir.AluOpType
+
+P = 128
+PACK = 4
+KP = P * PACK
+PASSES = K // KP
+NJ = 512
+HALVES = S // NJ
+MT = S2 // P
+PIECES = 0
+
+
+def tile_list_foster_dog_ease_kernel(
+    tc, tab_words, tab_scales, offs, offs2, w1, w4_words, w4_scales, ref, gain, house, visit, out
+):
+    nc = tc.nc
+    with ExitStack() as ctx:
+        keep = ctx.enter_context(tc.tile_pool(name="keep", bufs=1))
+        work = ctx.enter_context(tc.tile_pool(name="work", bufs=2))
+        psum = ctx.enter_context(tc.psum_pool(name="psum", bufs=1))
+
+        def kept(shape, dtype, name, tag=""):
+            return keep.tile(shape, dtype, name=name, tag=tag, align_bytes=64)
+
+        def streamed(shape, dtype, name):
+            return work.tile(shape, dtype, name=name, tag="stream", bufs=2)
+
+        idx = kept([P, S // 16], U16, "idx")
+        idx2 = kept([P, S2 // 16], U16, "idx2")
+        tab_w = [kept([P, T], U32, "tab_w%d" % a) for a in range(PASSES)]
+        tab_s = kept([P, T], U8, "tab_s")
+        w4s_raw = kept([P, PASSES, K], U8, "w4s_raw")
+        ref_sb = kept([P, PASSES, PACK], F32, "ref_sb")
+        gain_sb = kept([P, PASSES, PACK], F32, "gain_sb")
+        house_sb = kept([P, MT], F32, "house_sb")
+        v_s1 = kept([P, S], U8, "v_s1")
+        w1_raw = {}
+        visit_sb = {}
+
+        nc.gpsimd.memset(tab_s[:].bitcast(I32), 0)
+        nc.vector.memset(w4s_raw[:].rearrange("p a c -> p (a c)").bitcast(I32), 0)
+        nc.vector.memset(v_s1[:].bitcast(I32), 0)
+
+        def load_tab_words(a):
+            nc.sync.dma_start(
+                out=tab_w[a][:].bitcast(I32), in_=tab_words[a].rearrange("p t i -> p (t i)").bitcast(I32)
+            )
+
+        def load_w1(b, a):
+            rows = w1[a * KP : (a + 1) * KP, b * KP : (b + 1) * KP]
+            w1_raw[b, a] = streamed([P, PACK, KP], F32, "w1_raw")
+            nc.sync.dma_start(out=w1_raw[b, a][:], in_=rows.rearrange("(p j) c -> p j c", j=PACK))
+
+        def load_visit(c):
+            visit_sb[c] = streamed([P, MT, NJ], F32, "visit_sb")
+            nc.sync.dma_start(
+                out=visit_sb[c][:], in_=visit[:, c * NJ : (c + 1) * NJ].rearrange("(m p) c -> p m c", p=P)
+            )
+
+        nc.sync.dma_start(idx[:], offs)
+        nc.sync.dma_start(idx2[:], offs2)
+        nc.sync.dma_start(out=ref_sb[:], in_=ref.rearrange("(b p t) -> p b t", p=P, t=PACK))
+        load_tab_words(0)
+        for q in range(4):
+            nc.sync.dma_start(
+                out=tab_s[32 * q : 32 * q + 4 * PASSES, :].bitcast(I32),
+                in_=tab_scales[:, 4 * q : 4 * q + 4, :].bitcast(I32),
+            )
+        w4_raw = streamed([P, PASSES, 2 * K], U8, "w4_raw")
+        nc.sync.dma_start(out=w4_raw[:].bitcast(I32), in_=w4_words.rearrange("a p c -> p a c").bitcast(I32))
+        nc.sync.dma_start(out=gain_sb[:], in_=gain.rearrange("(b p t) -> p b t", p=P, t=PACK))
+        load_w1(0, 0)
+        for q in range(4):
+            nc.sync.dma_start(
+                out=w4s_raw[32 * q : 32 * q + 4, :, :].bitcast(I32),
+                in_=w4_scales[:, 4 * q : 4 * q + 4, :].rearrange("a r c -> r a c").bitcast(I32),
+            )
+        load_tab_words(1)
+        with nc.allow_non_contiguous_dma(reason="one factor for each output row, a row to a partition"):
+            nc.gpsimd.dma_start(out=house_sb[:], in_=house.rearrange("(m p) -> p m", p=P))
+
+        v_w = [[kept([P, NJ], U32, "v_w%d%d" % (a, c)) for c in range(HALVES)] for a in range(PASSES)]
+        v_s = kept([P, S], U8, "v_s")
+
+        def gather_v(a, c):
+            cols = NJ // 16
+            nc.vector.tensor_copy(v_w[a][c][:], tab_w[a][:].indirect(idx[:, c * cols : (c + 1) * cols]))
+
+        nc.vector.tensor_copy(v_s[:], tab_s[:].indirect(idx[:]))
+        for q in range(4):
+            nc.sync.dma_start(
+                out=v_s1[32 * q : 32 * q + 4, :].bitcast(I32), in_=v_s[32 * q + 4 : 32 * q + 8, :].bitcast(I32)
+            )
+        for c in range(HALVES):
+            gather_v(0, c)
+
+        w4_c = kept([P, 2 * PASSES * K], U8, "w4_c")
+        w4_s = kept([P, PASSES * K], U8, "w4_s")
+        nc.scalar.copy(
+            out=w4_c[:].bitcast(U16).rearrange("p (g t m) -> p g m t", t=PACK, m=P),
+            in_=w4_raw[:].rearrange("p a c -> p (a c)").bitcast(U16).rearrange("p (g m t) -> p g m t", t=PACK, m=P),
+        )
+        load_w1(0, 1)
+        nc.vector.tensor_copy(
+            out=w4_s[:].rearrange("p (g t m) -> p g m t", t=PACK, m=P),
+            in_=w4s_raw[:].rearrange("p a (b m t) -> p (a b) m t", t=PACK, m=P),
+        )
+        for c in range(HALVES):
+            gather_v(1, c)
+
+        w1_c = [[kept([P, KP], U32, "w1_c%d%d" % (b, a)) for a in range(PASSES)] for b in range(PASSES)]
+        w1_s = [[kept([P, KP], U8, "w1_s%d%d" % (b, a)) for a in range(PASSES)] for b in range(PASSES)]
+
+        def quantise_w1(b, a, shares):
+            grouped = kept([P, PACK * KP], BF16, "w1_bf", tag="w1_bf%d%d" % (b, a))
+            dst = grouped[:].rearrange("p (t m j) -> p m j t", t=PACK, j=PACK)
+            src = w1_raw[b, a][:].rearrange("p j (m t) -> p m j t", t=PACK)
+            for copy, m0, m1 in shares:
+                copy(out=dst[:, m0:m1], in_=src[:, m0:m1])
+            nc.vector.quantize_mx(out=w1_c[b][a][:].bitcast(FP8X4), scales=w1_s[b][a][:], in_=grouped[:])
+
+        dev = {}
+        h_c = {}
+        h_s = {}
+        planes = {}
+
+        def deviation(b, j0, n, t):
+            c, o = divmod(j0, NJ)
+            trait = psum.tile([P, n], F32, name="trait", bufs=2)
+            for a in range(PASSES):
+                col = a * K + b * KP + t * P
+                scales = v_s if a == 0 else v_s1
+                nc.tensor.matmul_mx(
+                    out=trait[:],
+                    lhsT=w4_c[:, 2 * col : 2 * (col + P)].bitcast(FP4X4),
+                    lhsT_scale=w4_s[:, col : col + P],
+                    rhs=v_w[a][c][:, o : o + n].bitcast(FP8X4),
+                    rhs_scale=scales[:, j0 : j0 + n],
+                    start=(a == 0),
+                    stop=(a == PASSES - 1),
+                )
+            dev[b, j0, t] = work.tile([P, n], F32, name="dev", bufs=4)
+            nc.scalar.activation(
+                out=dev[b, j0, t][:], in_=trait[:], func=ACT.Abs, bias=ref_sb[:, b, t : t + 1], scale=-1.0
+            )
+
+        def make_h(b, j0, n, between=()):
+            c, o = divmod(j0, NJ)
+            planes[b, j0] = work.tile([P, PACK, n], BF16, name="h_planes", align_bytes=64)
+            for t in range(PACK):
+                if (b, j0, t) not in dev:
+                    deviation(b, j0, n, t)
+                arg = psum.tile([P, n], F32, name="arg", bufs=3)
+                for a in range(PASSES):
+                    nc.tensor.matmul_mx(
+                        out=arg[:],
+                        lhsT=w1_c[b][a][:, t * P : (t + 1) * P].bitcast(FP8X4),
+                        lhsT_scale=w1_s[b][a][:, t * P : (t + 1) * P],
+                        rhs=v_w[a][c][:, o : o + n].bitcast(FP8X4),
+                        rhs_scale=v_s[4 * a : P, j0 : j0 + n],
+                        start=(a == 0),
+                        stop=(a == PASSES - 1),
+                    )
+                gate = work.tile([P, n], F32, name="gate", bufs=4)
+                nc.scalar.activation(out=gate[:], in_=arg[:], func=ACT.Sigmoid)
+                nc.vector.scalar_tensor_tensor(
+                    out=planes[b, j0][:, t, :],
+                    in0=dev[b, j0, t][:],
+                    scalar=gain_sb[:, b, t : t + 1],
+                    in1=gate[:],
+                    op0=ALU.mult,
+                    op1=ALU.mult,
+                )
+                if t < len(between):
+                    between[t]()
+
+        wovens = {}
+
+        def weave_h(b, j0, n, copy):
+            wovens[b, j0] = work.tile([P, PACK * n], BF16, name="h_woven", align_bytes=64)
+            copy(
+                out=wovens[b, j0][:].rearrange("p (c i t) -> p c t i", i=4, t=PACK),
+                in_=planes[b, j0][:].rearrange("p t (c i) -> p c t i", i=4),
+            )
+
+        def quantise_h(b, j0, n):
+            woven = wovens[b, j0]
+            h_c[b, j0] = kept([P, n], U32, "h_c%d_%d" % (b, j0))
+            h_s[b, j0] = kept([P, n], U8, "h_s%d_%d" % (b, j0))
+            nc.vector.quantize_mx(out=h_c[b, j0][:].bitcast(FP8X4), scales=h_s[b, j0][:], in_=woven[:])
+
+        def h_operand(b, j0, n):
+            start = max(s for (bb, s) in h_c if bb == b and s <= j0)
+            o = j0 - start
+            return h_c[b, start][:, o : o + n].bitcast(FP8X4), h_s[b, start][:, o : o + n]
+
+        def score(j0, n, tiles=range(MT)):
+            c, o = divmod(j0, NJ)
+            for m in tiles:
+                e = psum.tile([P, n], F32, name="e", bufs=3)
+                for b in range(PASSES):
+                    codes, scales = h_operand(b, j0, n)
+                    nc.tensor.matmul_mx(
+                        out=e[:],
+                        lhsT=v2_w[:, b, m * P : (m + 1) * P].bitcast(FP8X4),
+                        lhsT_scale=v2_s[4 * b : P, m * P : (m + 1) * P],
+                        rhs=codes,
+                        rhs_scale=scales,
+                        start=(b == 0),
+                        stop=(b == PASSES - 1),
+                    )
+                res = work.tile([P, n], F32, name="res", bufs=4)
+                nc.vector.scalar_tensor_tensor(
+                    out=res[:],
+                    in0=e[:],
+                    scalar=house_sb[:, m : m + 1],
+                    in1=visit_sb[c][:, m, o : o + n],
+                    op0=ALU.mult,
+                    op1=ALU.add,
+                )
+                nc.sync.dma_start(out=out[m * P : (m + 1) * P, j0 : j0 + n], in_=res[:])
+
+        on_scalar, on_vector, on_gpsimd = nc.scalar.copy, nc.vector.tensor_copy, nc.gpsimd.tensor_copy
+        quantise_w1(0, 0, [(on_scalar, 0, P)])
+        load_w1(1, 0)
+        quantise_w1(0, 1, [(on_scalar, 0, 64), (on_vector, 64, P)])
+        load_w1(1, 1)
+        v2_s = kept([P, S2], U8, "v2_s", tag="w1_bf00")
+        v2_w = kept([P, PASSES, S2], U32, "v2_w", tag="w1_bf01")
+
+        def gather_v2(a):
+            nc.vector.tensor_copy(v2_w[:, a, :], tab_w[a][:].indirect(idx2[:]))
+
+        def next_w1(a, shares):
+            quantise_w1(1, a, shares)
+            load_visit(a)
+
+        nc.vector.tensor_copy(v2_s[:], tab_s[:].indirect(idx2[:]))
+        gather_v2(0)
+        make_h(0, 0, NJ)
+        gather_v2(1)
+        make_h(0, NJ, NJ, [
+            lambda: weave_h(0, 0, NJ, on_vector),
+            lambda: next_w1(0, [(on_scalar, 0, P)]),
+            lambda: quantise_h(0, 0, NJ),
+            lambda: next_w1(1, [(on_scalar, 0, P)]),
+        ])
+        make_h(1, 0, NJ, [
+            lambda: weave_h(0, NJ, NJ, on_vector),
+            lambda: quantise_h(0, NJ, NJ),
+        ])
+        make_h(1, 512, 256, [
+            lambda: weave_h(1, 0, NJ, on_vector),
+            lambda: quantise_h(1, 0, NJ),
+        ])
+        make_h(1, 768, 256, [
+            lambda: weave_h(1, 512, 256, on_scalar),
+            lambda: score(0, NJ, [0]),
+            lambda: quantise_h(1, 512, 256),
+            lambda: score(0, NJ, [1]),
+        ])
+        weave_h(1, 768, 256, on_scalar)
+        score(0, NJ, [2, 3])
+        quantise_h(1, 768, 256)
+        score(512, 256)
+        score(768, 256)

@@ -39,16 +39,15 @@ def tile_list_foster_dog_ease_kernel(
             return keep.tile(shape, dtype, name=name, tag=tag, align_bytes=64)
 
         def streamed(shape, dtype, name):
-            return work.tile(shape, dtype, name=name, tag="stream", bufs=2)
+            return work.tile(shape, dtype, name=name, tag="stream", bufs=3)
 
         idx = kept([P, S // 16], U16, "idx")
         idx2 = kept([P, S2 // 16], U16, "idx2")
         tab_w = [kept([P, T], U32, "tab_w%d" % a) for a in range(PASSES)]
         tab_s = kept([P, T], U8, "tab_s")
-        w4s_raw = kept([P, PASSES, K], U8, "w4s_raw")
+        w4s_raw = kept([P, PASSES, K], U8, "w4s_raw", tag="w4s_raw")
         ref_sb = kept([P, PASSES, PACK], F32, "ref_sb")
         gain_sb = kept([P, PASSES, PACK], F32, "gain_sb")
-        house_sb = kept([P, MT], F32, "house_sb")
         v_s1 = kept([P, S], U8, "v_s1")
         w1_raw = {}
         visit_sb = {}
@@ -92,8 +91,7 @@ def tile_list_foster_dog_ease_kernel(
                 in_=w4_scales[:, 4 * q : 4 * q + 4, :].rearrange("a r c -> r a c").bitcast(I32),
             )
         load_tab_words(1)
-        with nc.allow_non_contiguous_dma(reason="one factor for each output row, a row to a partition"):
-            nc.gpsimd.dma_start(out=house_sb[:], in_=house.rearrange("(m p) -> p m", p=P))
+        load_w1(0, 1)
 
         v_w = [[kept([P, NJ], U32, "v_w%d%d" % (a, c)) for c in range(HALVES)] for a in range(PASSES)]
         v_s = kept([P, S], U8, "v_s")
@@ -103,12 +101,7 @@ def tile_list_foster_dog_ease_kernel(
             nc.vector.tensor_copy(v_w[a][c][:], tab_w[a][:].indirect(idx[:, c * cols : (c + 1) * cols]))
 
         nc.vector.tensor_copy(v_s[:], tab_s[:].indirect(idx[:]))
-        for q in range(4):
-            nc.sync.dma_start(
-                out=v_s1[32 * q : 32 * q + 4, :].bitcast(I32), in_=v_s[32 * q + 4 : 32 * q + 8, :].bitcast(I32)
-            )
-        for c in range(HALVES):
-            gather_v(0, c)
+        gather_v(0, 0)
 
         w4_c = kept([P, 2 * PASSES * K], U8, "w4_c")
         w4_s = kept([P, PASSES * K], U8, "w4_s")
@@ -116,13 +109,11 @@ def tile_list_foster_dog_ease_kernel(
             out=w4_c[:].bitcast(U16).rearrange("p (g t m) -> p g m t", t=PACK, m=P),
             in_=w4_raw[:].rearrange("p a c -> p (a c)").bitcast(U16).rearrange("p (g m t) -> p g m t", t=PACK, m=P),
         )
-        load_w1(0, 1)
         nc.vector.tensor_copy(
             out=w4_s[:].rearrange("p (g t m) -> p g m t", t=PACK, m=P),
             in_=w4s_raw[:].rearrange("p a (b m t) -> p (a b) m t", t=PACK, m=P),
         )
-        for c in range(HALVES):
-            gather_v(1, c)
+        gather_v(1, 0)
 
         w1_c = [[kept([P, KP], U32, "w1_c%d%d" % (b, a)) for a in range(PASSES)] for b in range(PASSES)]
         w1_s = [[kept([P, KP], U8, "w1_s%d%d" % (b, a)) for a in range(PASSES)] for b in range(PASSES)]
@@ -134,6 +125,12 @@ def tile_list_foster_dog_ease_kernel(
             for copy, m0, m1 in shares:
                 copy(out=dst[:, m0:m1], in_=src[:, m0:m1])
             nc.vector.quantize_mx(out=w1_c[b][a][:].bitcast(FP8X4), scales=w1_s[b][a][:], in_=grouped[:])
+
+        def move_scales():
+            for q in range(4):
+                nc.sync.dma_start(
+                    out=v_s1[32 * q : 32 * q + 4, :].bitcast(I32), in_=v_s[32 * q + 4 : 32 * q + 8, :].bitcast(I32)
+                )
 
         dev = {}
         h_c = {}
@@ -155,7 +152,7 @@ def tile_list_foster_dog_ease_kernel(
                     start=(a == 0),
                     stop=(a == PASSES - 1),
                 )
-            dev[b, j0, t] = work.tile([P, n], F32, name="dev", bufs=4)
+            dev[b, j0, t] = work.tile([P, n], F32, name="dev", bufs=8)
             nc.scalar.activation(
                 out=dev[b, j0, t][:], in_=trait[:], func=ACT.Abs, bias=ref_sb[:, b, t : t + 1], scale=-1.0
             )
@@ -177,7 +174,7 @@ def tile_list_foster_dog_ease_kernel(
                         start=(a == 0),
                         stop=(a == PASSES - 1),
                     )
-                gate = work.tile([P, n], F32, name="gate", bufs=4)
+                gate = work.tile([P, n], F32, name="gate", bufs=6)
                 nc.scalar.activation(out=gate[:], in_=arg[:], func=ACT.Sigmoid)
                 nc.vector.scalar_tensor_tensor(
                     out=planes[b, j0][:, t, :],
@@ -225,7 +222,7 @@ def tile_list_foster_dog_ease_kernel(
                         start=(b == 0),
                         stop=(b == PASSES - 1),
                     )
-                res = work.tile([P, n], F32, name="res", bufs=4)
+                res = work.tile([P, n], F32, name="res", bufs=12)
                 nc.vector.scalar_tensor_tensor(
                     out=res[:],
                     in0=e[:],
@@ -237,46 +234,58 @@ def tile_list_foster_dog_ease_kernel(
                 nc.sync.dma_start(out=out[m * P : (m + 1) * P, j0 : j0 + n], in_=res[:])
 
         on_scalar, on_vector, on_gpsimd = nc.scalar.copy, nc.vector.tensor_copy, nc.gpsimd.tensor_copy
+        move_scales()
         quantise_w1(0, 0, [(on_scalar, 0, P)])
         load_w1(1, 0)
-        quantise_w1(0, 1, [(on_scalar, 0, 64), (on_vector, 64, P)])
         load_w1(1, 1)
+        quantise_w1(0, 1, [(on_scalar, 0, P)])
+        house_sb = kept([P, MT], F32, "house_sb", tag="w4s_raw")
+        with nc.allow_non_contiguous_dma(reason="one factor for each output row, a row to a partition"):
+            nc.sync.dma_start(out=house_sb[:], in_=house.rearrange("(m p) -> p m", p=P))
+        load_visit(0)
         v2_s = kept([P, S2], U8, "v2_s", tag="w1_bf00")
         v2_w = kept([P, PASSES, S2], U32, "v2_w", tag="w1_bf01")
 
         def gather_v2(a):
             nc.vector.tensor_copy(v2_w[:, a, :], tab_w[a][:].indirect(idx2[:]))
 
-        def next_w1(a, shares):
-            quantise_w1(1, a, shares)
-            load_visit(a)
+        def nothing():
+            pass
 
-        nc.vector.tensor_copy(v2_s[:], tab_s[:].indirect(idx2[:]))
-        gather_v2(0)
-        make_h(0, 0, NJ)
-        gather_v2(1)
-        make_h(0, NJ, NJ, [
-            lambda: weave_h(0, 0, NJ, on_vector),
-            lambda: next_w1(0, [(on_scalar, 0, P)]),
-            lambda: quantise_h(0, 0, NJ),
-            lambda: next_w1(1, [(on_scalar, 0, P)]),
+        gather_v(0, 1)
+        gather_v(1, 1)
+        make_h(0, 0, NJ, [
+            lambda: quantise_w1(1, 0, [(on_vector, 0, P)]),
+            nothing,
+            lambda: quantise_w1(1, 1, [(on_vector, 0, P)]),
         ])
+        load_visit(1)
+        nc.vector.tensor_copy(v2_s[:], tab_s[:].indirect(idx2[:]))
         make_h(1, 0, NJ, [
-            lambda: weave_h(0, NJ, NJ, on_vector),
-            lambda: quantise_h(0, NJ, NJ),
+            lambda: weave_h(0, 0, NJ, on_vector),
+            lambda: gather_v2(0),
+            lambda: quantise_h(0, 0, NJ),
+            lambda: gather_v2(1),
+        ])
+        make_h(0, NJ, NJ, [
+            lambda: weave_h(1, 0, NJ, on_vector),
+            nothing,
+            lambda: quantise_h(1, 0, NJ),
+            lambda: score(0, NJ, [0]),
         ])
         make_h(1, 512, 256, [
-            lambda: weave_h(1, 0, NJ, on_vector),
-            lambda: quantise_h(1, 0, NJ),
+            lambda: weave_h(0, NJ, NJ, on_vector),
+            lambda: score(0, NJ, [1]),
+            lambda: quantise_h(0, NJ, NJ),
+            lambda: score(0, NJ, [2]),
         ])
         make_h(1, 768, 256, [
             lambda: weave_h(1, 512, 256, on_scalar),
-            lambda: score(0, NJ, [0]),
+            lambda: score(0, NJ, [3]),
             lambda: quantise_h(1, 512, 256),
-            lambda: score(0, NJ, [1]),
         ])
         weave_h(1, 768, 256, on_scalar)
-        score(0, NJ, [2, 3])
+        score(512, 256, [0, 1])
         quantise_h(1, 768, 256)
-        score(512, 256)
+        score(512, 256, [2, 3])
         score(768, 256)

@@ -45,7 +45,7 @@ def tile_list_foster_dog_ease_kernel(
         idx2 = kept([P, S2 // 16], U16, "idx2")
         tab_w = [kept([P, T], U32, "tab_w%d" % a) for a in range(PASSES)]
         tab_s = kept([P, T], U8, "tab_s")
-        w4s_raw = kept([P, PASSES, K], U8, "w4s_raw", tag="w4s_raw")
+        w4s_raw = kept([P, PASSES, K], U8, "w4s_raw")
         ref_sb = kept([P, PASSES, PACK], F32, "ref_sb")
         gain_sb = kept([P, PASSES, PACK], F32, "gain_sb")
         v_s1 = kept([P, S], U8, "v_s1")
@@ -119,7 +119,7 @@ def tile_list_foster_dog_ease_kernel(
         w1_s = [[kept([P, KP], U8, "w1_s%d%d" % (b, a)) for a in range(PASSES)] for b in range(PASSES)]
 
         def quantise_w1(b, a, shares):
-            grouped = kept([P, PACK * KP], BF16, "w1_bf", tag="w1_bf%d%d" % (b, a))
+            grouped = kept([P, PACK * KP], BF16, "w1_bf", tag="w1_bf%d" % (1 if b else a))
             dst = grouped[:].rearrange("p (t m j) -> p m j t", t=PACK, j=PACK)
             src = w1_raw[b, a][:].rearrange("p j (m t) -> p m j t", t=PACK)
             for copy, m0, m1 in shares:
@@ -174,7 +174,7 @@ def tile_list_foster_dog_ease_kernel(
                         start=(a == 0),
                         stop=(a == PASSES - 1),
                     )
-                gate = work.tile([P, n], F32, name="gate", bufs=6)
+                gate = work.tile([P, n], F32, name="gate", bufs=8)
                 nc.scalar.activation(out=gate[:], in_=arg[:], func=ACT.Sigmoid)
                 nc.vector.scalar_tensor_tensor(
                     out=planes[b, j0][:, t, :],
@@ -239,12 +239,12 @@ def tile_list_foster_dog_ease_kernel(
         load_w1(1, 0)
         load_w1(1, 1)
         quantise_w1(0, 1, [(on_scalar, 0, P)])
-        house_sb = kept([P, MT], F32, "house_sb", tag="w4s_raw")
+        house_sb = kept([P, MT], F32, "house_sb", tag="w1_bf0")
         with nc.allow_non_contiguous_dma(reason="one factor for each output row, a row to a partition"):
             nc.sync.dma_start(out=house_sb[:], in_=house.rearrange("(m p) -> p m", p=P))
         load_visit(0)
-        v2_s = kept([P, S2], U8, "v2_s", tag="w1_bf00")
-        v2_w = kept([P, PASSES, S2], U32, "v2_w", tag="w1_bf01")
+        v2_s = kept([P, S2], U8, "v2_s")
+        v2_w = kept([P, PASSES, S2], U32, "v2_w")
 
         def gather_v2(a):
             nc.vector.tensor_copy(v2_w[:, a, :], tab_w[a][:].indirect(idx2[:]))
@@ -254,37 +254,36 @@ def tile_list_foster_dog_ease_kernel(
 
         gather_v(0, 1)
         gather_v(1, 1)
-        make_h(0, 0, NJ, [
+        nc.vector.tensor_copy(v2_s[:], tab_s[:].indirect(idx2[:]))
+        gather_v2(0)
+        gather_v2(1)
+        make_h(0, 0, NJ)
+        make_h(0, NJ, NJ, [
+            lambda: weave_h(0, 0, NJ, on_vector),
             lambda: quantise_w1(1, 0, [(on_vector, 0, P)]),
-            nothing,
+            lambda: quantise_h(0, 0, NJ),
             lambda: quantise_w1(1, 1, [(on_vector, 0, P)]),
         ])
         load_visit(1)
-        nc.vector.tensor_copy(v2_s[:], tab_s[:].indirect(idx2[:]))
         make_h(1, 0, NJ, [
-            lambda: weave_h(0, 0, NJ, on_vector),
-            lambda: gather_v2(0),
-            lambda: quantise_h(0, 0, NJ),
-            lambda: gather_v2(1),
+            lambda: weave_h(0, NJ, NJ, on_vector),
+            nothing,
+            lambda: quantise_h(0, NJ, NJ),
         ])
-        make_h(0, NJ, NJ, [
+        make_h(1, 512, 256, [
             lambda: weave_h(1, 0, NJ, on_vector),
             nothing,
             lambda: quantise_h(1, 0, NJ),
             lambda: score(0, NJ, [0]),
         ])
-        make_h(1, 512, 256, [
-            lambda: weave_h(0, NJ, NJ, on_vector),
-            lambda: score(0, NJ, [1]),
-            lambda: quantise_h(0, NJ, NJ),
-            lambda: score(0, NJ, [2]),
-        ])
         make_h(1, 768, 256, [
             lambda: weave_h(1, 512, 256, on_scalar),
-            lambda: score(0, NJ, [3]),
+            lambda: score(0, NJ, [1]),
             lambda: quantise_h(1, 512, 256),
+            lambda: score(0, NJ, [2]),
         ])
         weave_h(1, 768, 256, on_scalar)
+        score(0, NJ, [3])
         score(512, 256, [0, 1])
         quantise_h(1, 768, 256)
         score(512, 256, [2, 3])

@@ -45,7 +45,7 @@ def tile_list_foster_dog_ease_kernel(
         idx2 = kept([P, S2 // 16], U16, "idx2")
         tab_w = [kept([P, T], U32, "tab_w%d" % a) for a in range(PASSES)]
         tab_s = kept([P, T], U8, "tab_s")
-        w4s_raw = kept([P, PASSES, K], U8, "w4s_raw")
+        w4s_raw = kept([P, PASSES, K], U8, "w4s_raw", tag="w4s_raw")
         ref_sb = kept([P, PASSES, PACK], F32, "ref_sb")
         gain_sb = kept([P, PASSES, PACK], F32, "gain_sb")
         v_s1 = kept([P, S], U8, "v_s1")
@@ -55,6 +55,10 @@ def tile_list_foster_dog_ease_kernel(
         nc.gpsimd.memset(tab_s[:].bitcast(I32), 0)
         nc.vector.memset(w4s_raw[:].rearrange("p a c -> p (a c)").bitcast(I32), 0)
         nc.vector.memset(v_s1[:].bitcast(I32), 0)
+
+        warm = kept([P, 16], F32, "warm")
+        nc.gpsimd.memset(warm[:, 0:1], 0.0)
+        nc.scalar.activation(out=warm[:, 8:9], in_=warm[:, 0:1], func=ACT.Sigmoid)
 
         def load_tab_words(a):
             nc.sync.dma_start(
@@ -116,10 +120,10 @@ def tile_list_foster_dog_ease_kernel(
         gather_v(1, 0)
 
         w1_c = [[kept([P, KP], U32, "w1_c%d%d" % (b, a)) for a in range(PASSES)] for b in range(PASSES)]
-        w1_s = [[kept([P, KP], U8, "w1_s%d%d" % (b, a)) for a in range(PASSES)] for b in range(PASSES)]
+        w1_s = [[kept([P, KP], U8, "w1_s%d%d" % (b, a), tag="w4s_raw" if (b, a) == (0, 0) else "") for a in range(PASSES)] for b in range(PASSES)]
 
         def quantise_w1(b, a, shares):
-            grouped = kept([P, PACK * KP], BF16, "w1_bf", tag="w1_bf%d" % (1 if b else a))
+            grouped = kept([P, PACK * KP], BF16, "w1_bf", tag="w1_bf%d%d" % (b, a))
             dst = grouped[:].rearrange("p (t m j) -> p m j t", t=PACK, j=PACK)
             src = w1_raw[b, a][:].rearrange("p j (m t) -> p m j t", t=PACK)
             for copy, m0, m1 in shares:
@@ -139,7 +143,7 @@ def tile_list_foster_dog_ease_kernel(
 
         def deviation(b, j0, n, t):
             c, o = divmod(j0, NJ)
-            trait = psum.tile([P, n], F32, name="trait", bufs=2)
+            trait = psum.tile([P, n], F32, name="trait", tag="bank", bufs=8)
             for a in range(PASSES):
                 col = a * K + b * KP + t * P
                 scales = v_s if a == 0 else v_s1
@@ -159,11 +163,11 @@ def tile_list_foster_dog_ease_kernel(
 
         def make_h(b, j0, n, between=()):
             c, o = divmod(j0, NJ)
-            planes[b, j0] = work.tile([P, PACK, n], BF16, name="h_planes", align_bytes=64)
+            planes[b, j0] = work.tile([P, PACK, n], BF16, name="h_planes", bufs=3, align_bytes=64)
             for t in range(PACK):
                 if (b, j0, t) not in dev:
                     deviation(b, j0, n, t)
-                arg = psum.tile([P, n], F32, name="arg", bufs=3)
+                arg = psum.tile([P, n], F32, name="arg", tag="bank", bufs=8)
                 for a in range(PASSES):
                     nc.tensor.matmul_mx(
                         out=arg[:],
@@ -191,10 +195,11 @@ def tile_list_foster_dog_ease_kernel(
 
         def weave_h(b, j0, n, copy):
             wovens[b, j0] = work.tile([P, PACK * n], BF16, name="h_woven", align_bytes=64)
-            copy(
-                out=wovens[b, j0][:].rearrange("p (c i t) -> p c t i", i=4, t=PACK),
-                in_=planes[b, j0][:].rearrange("p t (c i) -> p c t i", i=4),
-            )
+            dst = wovens[b, j0][:].rearrange("p (c i t) -> p c t i", i=4, t=PACK)
+            src = planes[b, j0][:].rearrange("p t (c i) -> p c t i", i=4)
+            groups = n // 4
+            for engine_copy, c0, c1 in copy:
+                engine_copy(out=dst[:, groups * c0 // P : groups * c1 // P], in_=src[:, groups * c0 // P : groups * c1 // P])
 
         def quantise_h(b, j0, n):
             woven = wovens[b, j0]
@@ -207,10 +212,11 @@ def tile_list_foster_dog_ease_kernel(
             o = j0 - start
             return h_c[b, start][:, o : o + n].bitcast(FP8X4), h_s[b, start][:, o : o + n]
 
-        def score(j0, n, tiles=range(MT)):
+        def score(j0, n, tiles):
             c, o = divmod(j0, NJ)
+            res = work.tile([P, len(tiles), n], F32, name="res", bufs=12)
             for m in tiles:
-                e = psum.tile([P, n], F32, name="e", bufs=3)
+                e = psum.tile([P, n], F32, name="e", tag="bank", bufs=8)
                 for b in range(PASSES):
                     codes, scales = h_operand(b, j0, n)
                     nc.tensor.matmul_mx(
@@ -222,29 +228,30 @@ def tile_list_foster_dog_ease_kernel(
                         start=(b == 0),
                         stop=(b == PASSES - 1),
                     )
-                res = work.tile([P, n], F32, name="res", bufs=12)
                 nc.vector.scalar_tensor_tensor(
-                    out=res[:],
+                    out=res[:, m - tiles[0], :],
                     in0=e[:],
                     scalar=house_sb[:, m : m + 1],
                     in1=visit_sb[c][:, m, o : o + n],
                     op0=ALU.mult,
                     op1=ALU.add,
                 )
-                nc.sync.dma_start(out=out[m * P : (m + 1) * P, j0 : j0 + n], in_=res[:])
+            rows = out[tiles[0] * P : (tiles[-1] + 1) * P, j0 : j0 + n]
+            nc.sync.dma_start(out=rows.rearrange("(m p) c -> p m c", p=P), in_=res[:])
 
-        on_scalar, on_vector, on_gpsimd = nc.scalar.copy, nc.vector.tensor_copy, nc.gpsimd.tensor_copy
+        on_scalar, on_vector = nc.scalar.copy, nc.vector.tensor_copy
+
+        def on_gpsimd(out, in_):
+            nc.gpsimd.tensor_scalar(out=out, in0=in_, scalar1=1.0, scalar2=0.0, op0=ALU.mult, op1=ALU.add)
+
         move_scales()
         quantise_w1(0, 0, [(on_scalar, 0, P)])
         load_w1(1, 0)
         load_w1(1, 1)
         quantise_w1(0, 1, [(on_scalar, 0, P)])
-        house_sb = kept([P, MT], F32, "house_sb", tag="w1_bf0")
-        with nc.allow_non_contiguous_dma(reason="one factor for each output row, a row to a partition"):
-            nc.sync.dma_start(out=house_sb[:], in_=house.rearrange("(m p) -> p m", p=P))
         load_visit(0)
-        v2_s = kept([P, S2], U8, "v2_s")
-        v2_w = kept([P, PASSES, S2], U32, "v2_w")
+        v2_s = kept([P, S2], U8, "v2_s", tag="w1_bf01")
+        v2_w = kept([P, PASSES, S2], U32, "v2_w", tag="w1_bf00")
 
         def gather_v2(a):
             nc.vector.tensor_copy(v2_w[:, a, :], tab_w[a][:].indirect(idx2[:]))
@@ -254,37 +261,46 @@ def tile_list_foster_dog_ease_kernel(
 
         gather_v(0, 1)
         gather_v(1, 1)
+        make_h(0, 0, NJ, [
+            nothing,
+            lambda: quantise_w1(1, 0, [(on_scalar, 0, P)]),
+            nothing,
+            lambda: quantise_w1(1, 1, [(on_vector, 0, P)]),
+        ])
         nc.vector.tensor_copy(v2_s[:], tab_s[:].indirect(idx2[:]))
         gather_v2(0)
         gather_v2(1)
-        make_h(0, 0, NJ)
         make_h(0, NJ, NJ, [
-            lambda: weave_h(0, 0, NJ, on_vector),
-            lambda: quantise_w1(1, 0, [(on_vector, 0, P)]),
+            lambda: weave_h(0, 0, NJ, [(on_vector, 0, P)]),
+            nothing,
             lambda: quantise_h(0, 0, NJ),
-            lambda: quantise_w1(1, 1, [(on_vector, 0, P)]),
+            nothing,
         ])
+        house_sb = kept([P, MT], F32, "house_sb", tag="w1_bf10")
+        with nc.allow_non_contiguous_dma(reason="one factor for each output row, a row to a partition"):
+            nc.sync.dma_start(out=house_sb[:], in_=house.rearrange("(m p) -> p m", p=P))
         load_visit(1)
         make_h(1, 0, NJ, [
-            lambda: weave_h(0, NJ, NJ, on_vector),
+            lambda: weave_h(0, NJ, NJ, [(on_vector, 0, P)]),
             nothing,
             lambda: quantise_h(0, NJ, NJ),
         ])
         make_h(1, 512, 256, [
-            lambda: weave_h(1, 0, NJ, on_vector),
+            lambda: weave_h(1, 0, NJ, [(on_vector, 0, P)]),
             nothing,
             lambda: quantise_h(1, 0, NJ),
-            lambda: score(0, NJ, [0]),
         ])
         make_h(1, 768, 256, [
-            lambda: weave_h(1, 512, 256, on_scalar),
-            lambda: score(0, NJ, [1]),
-            lambda: quantise_h(1, 512, 256),
-            lambda: score(0, NJ, [2]),
+            lambda: weave_h(1, 512, 256, [(on_scalar, 0, P)]),
         ])
-        weave_h(1, 768, 256, on_scalar)
-        score(0, NJ, [3])
-        score(512, 256, [0, 1])
+        weave_h(1, 768, 256, [(on_scalar, 0, P)])
+        quantise_h(1, 512, 256)
+        for g in [[0],[1]]:
+            score(0, NJ, g)
         quantise_h(1, 768, 256)
-        score(512, 256, [2, 3])
-        score(768, 256)
+        for g in [[2],[3]]:
+            score(0, NJ, g)
+        for g in [[0,1],[2,3]]:
+            score(512, 256, g)
+        for g in [[0,1],[2,3]]:
+            score(768, 256, g)

from contextlib import ExitStack

import concourse.mybir as mybir

K, T, S, S2 = 1024, 2048, 1024, 512
FLOPS = 2 * K * K * S * 2 + 2 * K * S2 * S

F32 = mybir.dt.float32
BF16 = mybir.dt.bfloat16
I32 = mybir.dt.int32
U32 = mybir.dt.uint32
U16 = mybir.dt.uint16
U8 = mybir.dt.uint8
FP8X4 = mybir.dt.float8_e4m3fn_x4
FP4X4 = mybir.dt.float4_e2m1fn_x4
ACT = mybir.ActivationFunctionType
ALU = mybir.AluOpType

P = 128
PACK = 4
KP = P * PACK
PASSES = K // KP
NJ = 512
HALVES = S // NJ
MT = S2 // P
PIECES = 0


def tile_list_foster_dog_ease_kernel(
    tc, tab_words, tab_scales, offs, offs2, w1, w4_words, w4_scales, ref, gain, house, visit, out
):
    nc = tc.nc
    with ExitStack() as ctx:
        keep = ctx.enter_context(tc.tile_pool(name="keep", bufs=1))
        work = ctx.enter_context(tc.tile_pool(name="work", bufs=2))
        psum = ctx.enter_context(tc.psum_pool(name="psum", bufs=1))

        def kept(shape, dtype, name, tag=""):
            return keep.tile(shape, dtype, name=name, tag=tag, align_bytes=64)

        def streamed(shape, dtype, name):
            return work.tile(shape, dtype, name=name, tag="stream", bufs=3)

        idx = kept([P, S // 16], U16, "idx")
        idx2 = kept([P, S2 // 16], U16, "idx2")
        tab_w = [kept([P, T], U32, "tab_w%d" % a) for a in range(PASSES)]
        tab_s = kept([P, T], U8, "tab_s")
        w4s_raw = kept([P, PASSES, K], U8, "w4s_raw", tag="w4s_raw")
        ref_sb = kept([P, PASSES, PACK], F32, "ref_sb")
        gain_sb = kept([P, PASSES, PACK], F32, "gain_sb")
        v_s1 = kept([P, S], U8, "v_s1")
        w1_raw = {}
        visit_sb = {}

        nc.gpsimd.memset(tab_s[:].bitcast(I32), 0)
        nc.vector.memset(w4s_raw[:].rearrange("p a c -> p (a c)").bitcast(I32), 0)
        nc.vector.memset(v_s1[:].bitcast(I32), 0)

        warm = kept([P, 16], F32, "warm")
        nc.gpsimd.memset(warm[:, 0:1], 0.0)
        nc.scalar.activation(out=warm[:, 8:9], in_=warm[:, 0:1], func=ACT.Sigmoid)

        def load_tab_words(a):
            nc.sync.dma_start(
                out=tab_w[a][:].bitcast(I32), in_=tab_words[a].rearrange("p t i -> p (t i)").bitcast(I32)
            )

        def load_w1(b, a):
            rows = w1[a * KP : (a + 1) * KP, b * KP : (b + 1) * KP]
            w1_raw[b, a] = streamed([P, PACK, KP], F32, "w1_raw")
            nc.sync.dma_start(out=w1_raw[b, a][:], in_=rows.rearrange("(p j) c -> p j c", j=PACK))

        def load_visit(c):
            visit_sb[c] = streamed([P, MT, NJ], F32, "visit_sb")
            nc.sync.dma_start(
                out=visit_sb[c][:], in_=visit[:, c * NJ : (c + 1) * NJ].rearrange("(m p) c -> p m c", p=P)
            )

        nc.sync.dma_start(idx[:], offs)
        nc.sync.dma_start(idx2[:], offs2)
        nc.sync.dma_start(out=ref_sb[:], in_=ref.rearrange("(b p t) -> p b t", p=P, t=PACK))
        load_tab_words(0)
        for q in range(4):
            nc.sync.dma_start(
                out=tab_s[32 * q : 32 * q + 4 * PASSES, :].bitcast(I32),
                in_=tab_scales[:, 4 * q : 4 * q + 4, :].bitcast(I32),
            )
        w4_raw = streamed([P, PASSES, 2 * K], U8, "w4_raw")
        nc.sync.dma_start(out=w4_raw[:].bitcast(I32), in_=w4_words.rearrange("a p c -> p a c").bitcast(I32))
        nc.sync.dma_start(out=gain_sb[:], in_=gain.rearrange("(b p t) -> p b t", p=P, t=PACK))
        load_w1(0, 0)
        for q in range(4):
            nc.sync.dma_start(
                out=w4s_raw[32 * q : 32 * q + 4, :, :].bitcast(I32),
                in_=w4_scales[:, 4 * q : 4 * q + 4, :].rearrange("a r c -> r a c").bitcast(I32),
            )
        load_tab_words(1)
        load_w1(0, 1)

        v_w = [[kept([P, NJ], U32, "v_w%d%d" % (a, c)) for c in range(HALVES)] for a in range(PASSES)]
        v_s = kept([P, S], U8, "v_s")

        def gather_v(a, c):
            cols = NJ // 16
            nc.vector.tensor_copy(v_w[a][c][:], tab_w[a][:].indirect(idx[:, c * cols : (c + 1) * cols]))

        nc.vector.tensor_copy(v_s[:], tab_s[:].indirect(idx[:]))
        gather_v(0, 0)

        w4_c = kept([P, 2 * PASSES * K], U8, "w4_c")
        w4_s = kept([P, PASSES * K], U8, "w4_s")
        nc.scalar.copy(
            out=w4_c[:].bitcast(U16).rearrange("p (g t m) -> p g m t", t=PACK, m=P),
            in_=w4_raw[:].rearrange("p a c -> p (a c)").bitcast(U16).rearrange("p (g m t) -> p g m t", t=PACK, m=P),
        )
        nc.vector.tensor_copy(
            out=w4_s[:].rearrange("p (g t m) -> p g m t", t=PACK, m=P),
            in_=w4s_raw[:].rearrange("p a (b m t) -> p (a b) m t", t=PACK, m=P),
        )
        gather_v(1, 0)

        w1_c = [[kept([P, KP], U32, "w1_c%d%d" % (b, a)) for a in range(PASSES)] for b in range(PASSES)]
        w1_s = [[kept([P, KP], U8, "w1_s%d%d" % (b, a), tag="w4s_raw" if (b, a) == (0, 0) else "") for a in range(PASSES)] for b in range(PASSES)]

        def quantise_w1(b, a, shares):
            grouped = kept([P, PACK * KP], BF16, "w1_bf", tag="w1_bf%d%d" % (b, a))
            dst = grouped[:].rearrange("p (t m j) -> p m j t", t=PACK, j=PACK)
            src = w1_raw[b, a][:].rearrange("p j (m t) -> p m j t", t=PACK)
            for copy, m0, m1 in shares:
                copy(out=dst[:, m0:m1], in_=src[:, m0:m1])
            nc.vector.quantize_mx(out=w1_c[b][a][:].bitcast(FP8X4), scales=w1_s[b][a][:], in_=grouped[:])

        def move_scales():
            for q in range(4):
                nc.sync.dma_start(
                    out=v_s1[32 * q : 32 * q + 4, :].bitcast(I32), in_=v_s[32 * q + 4 : 32 * q + 8, :].bitcast(I32)
                )

        dev = {}
        h_c = {}
        h_s = {}
        planes = {}

        def deviation(b, j0, n, t):
            c, o = divmod(j0, NJ)
            trait = psum.tile([P, n], F32, name="trait", tag="bank", bufs=8)
            for a in range(PASSES):
                col = a * K + b * KP + t * P
                scales = v_s if a == 0 else v_s1
                nc.tensor.matmul_mx(
                    out=trait[:],
                    lhsT=w4_c[:, 2 * col : 2 * (col + P)].bitcast(FP4X4),
                    lhsT_scale=w4_s[:, col : col + P],
                    rhs=v_w[a][c][:, o : o + n].bitcast(FP8X4),
                    rhs_scale=scales[:, j0 : j0 + n],
                    start=(a == 0),
                    stop=(a == PASSES - 1),
                )
            dev[b, j0, t] = work.tile([P, n], F32, name="dev", bufs=8)
            nc.scalar.activation(
                out=dev[b, j0, t][:], in_=trait[:], func=ACT.Abs, bias=ref_sb[:, b, t : t + 1], scale=-1.0
            )

        def make_h(b, j0, n, between=()):
            c, o = divmod(j0, NJ)
            planes[b, j0] = work.tile([P, PACK, n], BF16, name="h_planes", bufs=3, align_bytes=64)
            for t in range(PACK):
                if (b, j0, t) not in dev:
                    deviation(b, j0, n, t)
                arg = psum.tile([P, n], F32, name="arg", tag="bank", bufs=8)
                for a in range(PASSES):
                    nc.tensor.matmul_mx(
                        out=arg[:],
                        lhsT=w1_c[b][a][:, t * P : (t + 1) * P].bitcast(FP8X4),
                        lhsT_scale=w1_s[b][a][:, t * P : (t + 1) * P],
                        rhs=v_w[a][c][:, o : o + n].bitcast(FP8X4),
                        rhs_scale=v_s[4 * a : P, j0 : j0 + n],
                        start=(a == 0),
                        stop=(a == PASSES - 1),
                    )
                gate = work.tile([P, n], F32, name="gate", bufs=8)
                nc.scalar.activation(out=gate[:], in_=arg[:], func=ACT.Sigmoid)
                nc.vector.scalar_tensor_tensor(
                    out=planes[b, j0][:, t, :],
                    in0=dev[b, j0, t][:],
                    scalar=gain_sb[:, b, t : t + 1],
                    in1=gate[:],
                    op0=ALU.mult,
                    op1=ALU.mult,
                )
                if t < len(between):
                    between[t]()

        wovens = {}

        def weave_h(b, j0, n, copy):
            wovens[b, j0] = work.tile([P, PACK * n], BF16, name="h_woven", align_bytes=64)
            dst = wovens[b, j0][:].rearrange("p (c i t) -> p c t i", i=4, t=PACK)
            src = planes[b, j0][:].rearrange("p t (c i) -> p c t i", i=4)
            groups = n // 4
            for engine_copy, c0, c1 in copy:
                engine_copy(out=dst[:, groups * c0 // P : groups * c1 // P], in_=src[:, groups * c0 // P : groups * c1 // P])

        def quantise_h(b, j0, n):
            woven = wovens[b, j0]
            h_c[b, j0] = kept([P, n], U32, "h_c%d_%d" % (b, j0))
            h_s[b, j0] = kept([P, n], U8, "h_s%d_%d" % (b, j0))
            nc.vector.quantize_mx(out=h_c[b, j0][:].bitcast(FP8X4), scales=h_s[b, j0][:], in_=woven[:])

        def h_operand(b, j0, n):
            start = max(s for (bb, s) in h_c if bb == b and s <= j0)
            o = j0 - start
            return h_c[b, start][:, o : o + n].bitcast(FP8X4), h_s[b, start][:, o : o + n]

        def score(j0, n, tiles):
            c, o = divmod(j0, NJ)
            res = work.tile([P, len(tiles), n], F32, name="res", bufs=12)
            for m in tiles:
                e = psum.tile([P, n], F32, name="e", tag="bank", bufs=8)
                for b in range(PASSES):
                    codes, scales = h_operand(b, j0, n)
                    nc.tensor.matmul_mx(
                        out=e[:],
                        lhsT=v2_w[:, b, m * P : (m + 1) * P].bitcast(FP8X4),
                        lhsT_scale=v2_s[4 * b : P, m * P : (m + 1) * P],
                        rhs=codes,
                        rhs_scale=scales,
                        start=(b == 0),
                        stop=(b == PASSES - 1),
                    )
                nc.vector.scalar_tensor_tensor(
                    out=res[:, m - tiles[0], :],
                    in0=e[:],
                    scalar=house_sb[:, m : m + 1],
                    in1=visit_sb[c][:, m, o : o + n],
                    op0=ALU.mult,
                    op1=ALU.add,
                )
            rows = out[tiles[0] * P : (tiles[-1] + 1) * P, j0 : j0 + n]
            nc.sync.dma_start(out=rows.rearrange("(m p) c -> p m c", p=P), in_=res[:])

        on_scalar, on_vector = nc.scalar.copy, nc.vector.tensor_copy

        def on_gpsimd(out, in_):
            nc.gpsimd.tensor_scalar(out=out, in0=in_, scalar1=1.0, scalar2=0.0, op0=ALU.mult, op1=ALU.add)

        move_scales()
        quantise_w1(0, 0, [(on_scalar, 0, P)])
        load_w1(1, 0)
        load_w1(1, 1)
        quantise_w1(0, 1, [(on_scalar, 0, P)])
        load_visit(0)
        v2_s = kept([P, S2], U8, "v2_s", tag="w1_bf01")
        v2_w = kept([P, PASSES, S2], U32, "v2_w", tag="w1_bf00")

        def gather_v2(a):
            nc.vector.tensor_copy(v2_w[:, a, :], tab_w[a][:].indirect(idx2[:]))

        def nothing():
            pass

        gather_v(0, 1)
        gather_v(1, 1)
        make_h(0, 0, NJ, [
            nothing,
            lambda: quantise_w1(1, 0, [(on_scalar, 0, P)]),
            nothing,
            lambda: quantise_w1(1, 1, [(on_vector, 0, P)]),
        ])
        nc.vector.tensor_copy(v2_s[:], tab_s[:].indirect(idx2[:]))
        gather_v2(0)
        gather_v2(1)
        make_h(0, NJ, NJ, [
            lambda: weave_h(0, 0, NJ, [(on_vector, 0, P)]),
            nothing,
            lambda: quantise_h(0, 0, NJ),
            nothing,
        ])
        house_sb = kept([P, MT], F32, "house_sb", tag="w1_bf10")
        with nc.allow_non_contiguous_dma(reason="one factor for each output row, a row to a partition"):
            nc.sync.dma_start(out=house_sb[:], in_=house.rearrange("(m p) -> p m", p=P))
        load_visit(1)
        make_h(1, 0, NJ, [
            lambda: weave_h(0, NJ, NJ, [(on_vector, 0, P)]),
            nothing,
            lambda: quantise_h(0, NJ, NJ),
        ])
        make_h(1, 512, 256, [
            lambda: weave_h(1, 0, NJ, [(on_vector, 0, P)]),
            nothing,
            lambda: quantise_h(1, 0, NJ),
        ])
        make_h(1, 768, 256, [
            lambda: weave_h(1, 512, 256, [(on_scalar, 0, P)]),
        ])
        weave_h(1, 768, 256, [(on_scalar, 0, P)])
        quantise_h(1, 512, 256)
        for g in [[0],[1]]:
            score(0, NJ, g)
        quantise_h(1, 768, 256)
        for g in [[2],[3]]:
            score(0, NJ, g)
        for g in [[0,1],[2,3]]:
            score(512, 256, g)
        for g in [[0,1],[2,3]]:
            score(768, 256, g)
